import numpy as np
import ml_dtypes


def mxq(x, axis, fmt="e4m3"):
    dtype, down = {"e4m3": (ml_dtypes.float8_e4m3fn, 7), "e5m2": (ml_dtypes.float8_e5m2, 14)}[fmt]
    v = np.moveaxis(np.asarray(x, np.float32).astype(ml_dtypes.bfloat16).astype(np.float64), axis, -1)
    blocks = v.reshape(v.shape[:-1] + (-1, 32))
    amax = np.abs(blocks).max(-1, keepdims=True)
    byte = np.maximum(np.where(amax > 0, np.frexp(amax)[1] - 1 + 127, 0) - down, 1)
    scale = np.exp2(byte - 127.0)
    codes = (blocks / scale).astype(np.float32).astype(dtype).astype(np.float64)
    return np.moveaxis((codes * scale).reshape(v.shape), -1, axis)


WIDE = False


def mx_kscale(k):
    if not WIDE:
        return np.ones(k)
    levels = np.array([10, -10, 5, -5, 0])
    if k % 512:
        return np.exp2(np.random.permutation(np.resize(levels, k // 32))).repeat(32)
    a = np.empty((k // 512, 16))
    for p in range(k // 512):
        a[p, :8] = np.random.permutation(np.resize(levels, 8))
        for g in range(8):
            far = levels[np.abs(levels - a[p, g]) >= 10]
            a[p, g + 8] = far[np.random.randint(len(far))]
    return np.exp2(a.ravel()).repeat(32)


def f64(x):
    return np.asarray(x).astype(np.float64)


def striped(idx):
    return np.tile(np.asarray(idx).reshape(-1, 16).T, (8, 1)).astype(np.uint16)


def unstriped(offs):
    return offs[:16].T.reshape(-1).astype(np.int64)


def striped8(idx):
    return np.asarray(idx).reshape(8, -1, 16).transpose(0, 2, 1).reshape(128, -1).astype(np.uint16)


def unstriped8(offs):
    return offs.reshape(8, 16, -1).transpose(0, 2, 1).reshape(8, -1).astype(np.int64)


def pick8(x, idx, run):
    r = np.arange(len(x))
    return x[r[:, None], idx[r % (8 * run) // run]]


E2M1 = np.array([0.0, 0.5, 1.0, 1.5, 2.0, 3.0, 4.0, 6.0, -0.0, -0.5, -1.0, -1.5, -2.0, -3.0, -4.0, -6.0])


def pack_weight(w, fmt):
    k, n = w.shape
    w = f64(np.asarray(w, np.float32).astype(ml_dtypes.bfloat16)).reshape(k // 32, 32, n)
    amax = np.abs(w).max(1)
    if fmt == "e4m3":
        byte = np.frexp(amax)[1] - 1 + 127 - 7
    else:
        mant, ex = np.frexp(amax / 6.0)
        byte = np.where(mant > 0.5, ex, ex - 1) + 127
    byte = np.clip(np.where(amax > 0, byte, 1), 1, 254)
    scaled = (w * np.exp2(127.0 - byte)[:, None, :]).reshape(k, n).astype(np.float32)
    by_word = np.ascontiguousarray(scaled.reshape(k // 512, 128, 4, n).transpose(0, 1, 3, 2))
    if fmt == "e4m3":
        words = by_word.astype(ml_dtypes.float8_e4m3fn).view(np.uint8)
    else:
        c = by_word.astype(ml_dtypes.float4_e2m1fn).view(np.uint8) & 0xF
        words = (c[..., 0::2] | (c[..., 1::2] << 4)).reshape(k // 512, 128, 2 * n)
    return np.ascontiguousarray(words), np.ascontiguousarray(byte.astype(np.uint8).reshape(k // 512, 16, n))


def unpack_weight(words, scales, fmt):
    g, _, n = scales.shape
    words = np.ascontiguousarray(words).reshape(g, 128, n, -1)
    if fmt == "e4m3":
        vals = words.view(ml_dtypes.float8_e4m3fn).astype(np.float64)
    else:
        nib = np.empty((g, 128, n, 4), np.uint8)
        nib[..., 0::2] = words & 0xF
        nib[..., 1::2] = words >> 4
        vals = E2M1[nib]
    vals = vals * np.repeat(np.exp2(scales.astype(np.float64) - 127.0), 8, axis=1)[..., None]
    return vals.transpose(0, 1, 3, 2).reshape(g * 512, n)


def silu(v):
    return v / (1.0 + np.exp(-v))


def bf(x):
    return np.asarray(x, np.float32).astype(ml_dtypes.bfloat16)


def planes(Y):
    r, m = Y.shape
    b = f64(bf(Y)).reshape(r // 32, 32, m)
    amax = np.abs(b).max(1)
    byte = np.clip(np.where(amax > 0, np.frexp(amax)[1] - 1 + 127 - 7, 1), 1, 254)
    codes = (b * np.exp2(127.0 - byte)[:, None, :]).reshape(r, m).astype(np.float32).astype(ml_dtypes.float8_e4m3fn).view(np.uint8)
    words = codes.reshape(r // 512, 128, 4, m).transpose(0, 1, 3, 2)
    return np.ascontiguousarray(words), np.ascontiguousarray(byte.astype(np.uint8).reshape(r // 512, 16, m))


K, R, F, T, J, M, G = 512, 512, 512, 2048, 512, 128, 16


def setup_inputs():
    n = np.random.standard_normal
    idx = np.random.permutation(T)[:J]
    idx2 = np.stack([np.random.permutation(J)[:M] for _ in range(8)])
    fk = mx_kscale(K)
    fr = mx_kscale(R)
    tabp = pack_weight(n((K, T)) / fk[:, None], "e4m3")
    return {
        "tab_words": tabp[0],
        "tab_scales": tabp[1],
        "w1": (n((K, R)) * 1 / np.sqrt(K) * fk[:, None]).astype(np.float32),
        "gain": (np.random.uniform(0.5, 1.5, (R, 1))).astype(np.float32),
        "pb": (np.random.uniform(-0.7, 0.7, (1, M))).astype(np.float32),
        "rs": (np.random.uniform(0.5, 2.0, (R, 1)) * fr[:, None]).astype(np.float32),
        "wor": (n((R, F)) * 1 / np.sqrt(R) / fr[:, None]).astype(np.float32),
        "res": (n((F, M)) * 0.5).astype(np.float32),
        "offs": striped(idx),
        "offs2": striped8(idx2),
    }


def reference(tab_words, tab_scales, w1, gain, pb, rs, wor, res, offs, offs2):
    idx = unstriped(offs)
    idx2 = unstriped8(offs2)
    tabu = unpack_weight(tab_words, tab_scales, "e4m3")
    w1q = mxq(f64(w1), 0, "e4m3")
    tabidxg = tabu[:, idx]
    a = w1q.T @ tabidxg
    h1 = a * f64(gain)
    s = pick8(h1, idx2, 64) + f64(pb)
    q2 = np.sqrt(np.square(s).reshape(R, G, M // G).mean(axis=2) + 0.1)
    qr = np.repeat(q2, M // G, axis=1)
    u1 = silu(s / qr)
    fo1 = u1 * f64(rs)
    worq = mxq(f64(wor), 0, "e4m3")
    fo1q = mxq(fo1, 0, "e4m3")
    yo = worq.T @ fo1q
    y = yo + f64(res)
    words, scales = planes(y)
    return y, words, scales

@@ -1,0 +1,153 @@
+from contextlib import ExitStack
+
+import concourse.mybir as mybir
+
+K, R, F, T, J, M, G = 512, 512, 512, 2048, 512, 128, 16
+FLOPS = 2 * K * R * J + 2 * R * F * M
+
+F32 = mybir.dt.float32
+BF16 = mybir.dt.bfloat16
+I32 = mybir.dt.int32
+U32 = mybir.dt.uint32
+U16 = mybir.dt.uint16
+U8 = mybir.dt.uint8
+FP8X4 = mybir.dt.float8_e4m3fn_x4
+ACT = mybir.ActivationFunctionType
+ALU = mybir.AluOpType
+AX = mybir.AxisListType
+
+P = 128
+PACK = 4
+HALF = J // 2
+GROUP = M // G
+W1_VECTOR_COLS = 80
+
+
+def tile_attend_chpickscaled_pl_kernel(tc, tab_words, tab_scales, w1, gain, pb, rs, wor, res, offs, offs2, out_0, out_1, out_2):
+    nc = tc.nc
+    with ExitStack() as ctx:
+        sb = ctx.enter_context(tc.tile_pool(name="sb", bufs=1))
+        ps = ctx.enter_context(tc.psum_pool(name="ps", bufs=1))
+
+        def bank(b, cols):
+            return ps.tile([P, cols], F32, name="bank%d" % b, tag="bank%d" % b)
+
+        slots = sb.tile([P, J // 16], U16, name="slots")
+        nc.sync.dma_start(slots[:], offs)
+        tab_s = sb.tile([P, T], U8, name="tab_s", align_bytes=64)
+        nc.vector.memset(tab_s[:].bitcast(I32), 0)
+        w1_raw = sb.tile([P, PACK, R], F32, name="w1_raw")
+        w1_rows = w1.rearrange("(p j) c -> p j c", j=PACK)
+        nc.sync.dma_start(w1_raw[:, :2], w1_rows[:, :2])
+        for q in range(4):
+            nc.sync.dma_start(tab_s[32 * q : 32 * q + 4, :].bitcast(I32), tab_scales[0, 4 * q : 4 * q + 4, :].bitcast(I32))
+        nc.sync.dma_start(w1_raw[:, 2:], w1_rows[:, 2:])
+        tab_w = sb.tile([P, T], I32, name="tab_w", align_bytes=64)
+        nc.sync.dma_start(tab_w[:], tab_words[0].rearrange("p n t -> p (n t)").bitcast(I32))
+        picks = sb.tile([P, M // 16], U16, name="picks")
+        nc.sync.dma_start(picks[:], offs2)
+        gain_t = sb.tile([P, PACK], F32, name="gain_t")
+        nc.gpsimd.dma_start(gain_t[:], gain.rearrange("(p t) o -> p (t o)", t=PACK))
+        rs_t = sb.tile([P, PACK], F32, name="rs_t")
+        nc.gpsimd.dma_start(rs_t[:], rs.rearrange("(p t) o -> p (t o)", t=PACK))
+        pb_row = sb.tile([P, M], F32, name="pb_row")
+        nc.sync.dma_start(pb_row[:], pb[0].partition_broadcast(P))
+        wor_rows = wor.rearrange("(p j) c -> p j c", j=PACK)
+        wor_raw = []
+        for h in range(2):
+            part = sb.tile([P, PACK, F // 2], F32, name="wor_raw%d" % h)
+            nc.sync.dma_start(part[:], wor_rows[:, :, h * (F // 2) : (h + 1) * (F // 2)])
+            wor_raw.append(part)
+        res_t = sb.tile([P, PACK, M], F32, name="res_t")
+        nc.sync.dma_start(res_t[:], res.rearrange("(p t) m -> p t m", t=PACK))
+
+        warm = sb.tile([P, 1], F32, name="warm")
+        nc.vector.memset(warm[:], 1.0)
+        warm2 = sb.tile([P, 1], F32, name="warm2")
+        nc.scalar.activation(warm2[:], warm[:], ACT.Abs_reciprocal_sqrt)
+
+
+        g_s = sb.tile([P, J], U8, name="g_s", align_bytes=64)
+        nc.vector.tensor_copy(g_s[:], tab_s[:].indirect(slots[:]))
+
+        w1_b = sb.tile([P, PACK, P, PACK], BF16, name="w1_b", align_bytes=64)
+        src = w1_raw[:].rearrange("p j (m t) -> p m j t", t=PACK)
+        dst = w1_b[:].rearrange("p t m j -> p m j t")
+        nc.vector.tensor_copy(dst[:, :W1_VECTOR_COLS], src[:, :W1_VECTOR_COLS])
+        nc.scalar.copy(dst[:, W1_VECTOR_COLS:], src[:, W1_VECTOR_COLS:])
+        w1_c = sb.tile([P, R], U32, name="w1_c", align_bytes=64)
+        w1_s = sb.tile([P, R], U8, name="w1_s", align_bytes=64)
+        nc.vector.quantize_mx(w1_c[:].bitcast(FP8X4), w1_s[:], w1_b[:].rearrange("p t m j -> p (t m j)"))
+
+        g_w = []
+        for h in range(2):
+            part = sb.tile([P, HALF], U32, name="g_w%d" % h, align_bytes=64)
+            nc.vector.tensor_copy(part[:], tab_w[:].bitcast(U32).indirect(slots[:, h * HALF // 16 : (h + 1) * HALF // 16]))
+            g_w.append(part)
+
+        h1 = [sb.tile([P, J], F32, name="h1_%d" % t) for t in range(PACK)]
+        order = [(0, 0), (1, 0), (0, 1), (1, 1), (2, 0), (2, 1), (3, 0), (3, 1)]
+        for t, h in order:
+            acc = bank(2 * t + h, HALF)
+            nc.tensor.matmul_mx(
+                acc[:], lhsT=w1_c[:, t * P : (t + 1) * P].bitcast(FP8X4), lhsT_scale=w1_s[:, t * P : (t + 1) * P],
+                rhs=g_w[h][:].bitcast(FP8X4), rhs_scale=g_s[:, h * HALF : (h + 1) * HALF], start=True, stop=True)
+            nc.scalar.activation(h1[t][:, h * HALF : (h + 1) * HALF], acc[:], ACT.Copy, scale=gain_t[:, t : t + 1])
+
+        wor_b = sb.tile([P, PACK, P, PACK], BF16, name="wor_b", align_bytes=64)
+        wdst = wor_b[:].rearrange("p t m j -> p m j t")
+        nc.vector.tensor_copy(wdst[:, : P // 2], wor_raw[0][:].rearrange("p j (m t) -> p m j t", t=PACK))
+
+        s = sb.tile([P, PACK, M], F32, name="s")
+        sq_head = sb.tile([P, PACK - 1, M], F32, name="sq_head")
+        sq_last = wor_b[:].rearrange("p t m j -> p t (m j)")[:, 0:1, 2 * M :].bitcast(F32)
+        ssum = sb.tile([P, G, PACK], F32, name="ssum")
+        for t in range(PACK):
+            nc.vector.tensor_tensor(s[:, t, :], h1[t][:].indirect(picks[:]), pb_row[:], ALU.add)
+        for ts, sq in ((slice(0, PACK - 1), sq_head[:]), (slice(PACK - 1, PACK), sq_last)):
+            nc.scalar.activation(sq, s[:, ts, :], ACT.Square)
+            nc.vector.tensor_reduce(ssum[:].rearrange("p g t -> p t g")[:, ts], sq.rearrange("p t (g i) -> p t g i", i=GROUP), AX.X, ALU.add)
+        rinv = sb.tile([P, G, PACK], F32, name="rinv")
+        nc.scalar.activation(rinv[:], ssum[:], ACT.Abs_reciprocal_sqrt, bias=0.1, scale=1.0 / GROUP)
+
+        z = sb.tile([P, M, PACK], F32, name="z")
+        nc.vector.tensor_tensor(
+            z[:].rearrange("p (g i) t -> p g i t", i=GROUP),
+            s[:].rearrange("p t (g i) -> p g i t", i=GROUP),
+            rinv[:].unsqueeze(2).to_broadcast([P, G, GROUP, PACK]), ALU.mult)
+
+        nc.vector.tensor_copy(wdst[:, P // 2 :], wor_raw[1][:].rearrange("p j (m t) -> p m j t", t=PACK))
+        wor_c = sb.tile([P, F], U32, name="wor_c", align_bytes=64)
+        wor_s = sb.tile([P, F], U8, name="wor_s", align_bytes=64)
+        nc.vector.quantize_mx(wor_c[:].bitcast(FP8X4), wor_s[:], wor_b[:].rearrange("p t m j -> p (t m j)"))
+
+
+        u = sb.tile([P, M, PACK], F32, name="u")
+        fo_b = sb.tile([P, M, PACK], BF16, name="fo_b", align_bytes=64)
+        for h in range(2):
+            ms = slice(h * M // 2, (h + 1) * M // 2)
+            nc.scalar.activation(u[:, ms, :], z[:, ms, :], ACT.Silu)
+            nc.vector.tensor_tensor(fo_b[:, ms, :], u[:, ms, :], rs_t[:].unsqueeze(1).to_broadcast([P, M // 2, PACK]), ALU.mult)
+        fo_c = sb.tile([P, M], U32, name="fo_c", align_bytes=64)
+        fo_s = sb.tile([P, M], U8, name="fo_s", align_bytes=64)
+        nc.vector.quantize_mx(fo_c[:].bitcast(FP8X4), fo_s[:], fo_b[:].rearrange("p m t -> p (m t)"))
+
+        y = sb.tile([P, PACK, M], F32, name="y")
+        for t in range(PACK):
+            acc = bank(t, M)
+            nc.tensor.matmul_mx(
+                acc[:], lhsT=wor_c[:, t * P : (t + 1) * P].bitcast(FP8X4), lhsT_scale=wor_s[:, t * P : (t + 1) * P],
+                rhs=fo_c[:].bitcast(FP8X4), rhs_scale=fo_s[:], start=True, stop=True)
+            nc.vector.tensor_tensor(y[:, t, :], acc[:], res_t[:, t, :], ALU.add)
+        nc.scalar.dma_start(out_0.rearrange("(p t) m -> p t m", t=PACK), y[:])
+
+        y_b = sb.tile([P, M, PACK], BF16, name="y_b", align_bytes=64)
+        nc.vector.tensor_copy(
+            y_b[:].rearrange("p (c i) t -> p c t i", i=4), y[:].rearrange("p t (c i) -> p c t i", i=4))
+        y_c = sb.tile([P, M], U32, name="y_c", align_bytes=64)
+        y_s = sb.tile([P, M], U8, name="y_s", align_bytes=64)
+        nc.vector.quantize_mx(y_c[:].bitcast(FP8X4), y_s[:], y_b[:].rearrange("p m t -> p (m t)"))
+        nc.sync.dma_start(out_1[0].rearrange("p c r -> p (c r)").bitcast(I32), y_c[:].bitcast(I32))
+        for q in range(4):
+            eng = nc.sync if q < 2 else nc.scalar
+            eng.dma_start(out_2[0, 4 * q : 4 * q + 4, :].bitcast(I32), y_s[32 * q : 32 * q + 4, :].bitcast(I32))

@@ -1,6 +1,7 @@
 from contextlib import ExitStack
 
 import concourse.mybir as mybir
+from concourse.masks import make_identity
 
 K, R, F, T, J, M, G = 512, 512, 512, 2048, 512, 128, 16
 FLOPS = 2 * K * R * J + 2 * R * F * M
@@ -20,7 +21,7 @@ P = 128
 PACK = 4
 HALF = J // 2
 GROUP = M // G
-W1_VECTOR_COLS = 80
+W1_VECTOR_COLS = 40
 
 
 def tile_attend_chpickscaled_pl_kernel(tc, tab_words, tab_scales, w1, gain, pb, rs, wor, res, offs, offs2, out_0, out_1, out_2):
@@ -36,28 +37,33 @@ def tile_attend_chpickscaled_pl_kernel(tc, tab_words, tab_scales, w1, gain, pb, 
         nc.sync.dma_start(slots[:], offs)
         tab_s = sb.tile([P, T], U8, name="tab_s", align_bytes=64)
         nc.vector.memset(tab_s[:].bitcast(I32), 0)
-        w1_raw = sb.tile([P, PACK, R], F32, name="w1_raw")
-        w1_rows = w1.rearrange("(p j) c -> p j c", j=PACK)
-        nc.sync.dma_start(w1_raw[:, :2], w1_rows[:, :2])
+        tab_w = sb.tile([P, T], I32, name="tab_w", align_bytes=64)
+        words_hbm = tab_words[0].rearrange("p n t -> p (n t)").bitcast(I32)
+        nc.sync.dma_start(tab_w[:, : T // 2], words_hbm[:, : T // 2])
         for q in range(4):
             nc.sync.dma_start(tab_s[32 * q : 32 * q + 4, :].bitcast(I32), tab_scales[0, 4 * q : 4 * q + 4, :].bitcast(I32))
-        nc.sync.dma_start(w1_raw[:, 2:], w1_rows[:, 2:])
-        tab_w = sb.tile([P, T], I32, name="tab_w", align_bytes=64)
-        nc.sync.dma_start(tab_w[:], tab_words[0].rearrange("p n t -> p (n t)").bitcast(I32))
+        nc.sync.dma_start(tab_w[:, T // 2 :], words_hbm[:, T // 2 :])
+
+        def load_halves(w, name):
+            rows = w.rearrange("(p j) c -> p j c", j=PACK)
+            halves = []
+            for h in range(2):
+                part = sb.tile([P, PACK, R // 2], F32, name="%s%d" % (name, h))
+                nc.sync.dma_start(part[:], rows[:, :, h * (R // 2) : (h + 1) * (R // 2)])
+                halves.append(part)
+            return halves
+
+        w1_raw = load_halves(w1, "w1_raw")
+        pb_col = sb.tile([P, 1], F32, name="pb_col")
+        with nc.allow_non_contiguous_dma(reason="one value a partition"):
+            nc.sync.dma_start(pb_col[:], pb.rearrange("o m -> m o"))
+        gain_t = sb.tile([P, PACK], F32, name="gain_t")
+        nc.sync.dma_start(gain_t[:], gain.rearrange("(p t) o -> p (t o)", t=PACK))
         picks = sb.tile([P, M // 16], U16, name="picks")
         nc.sync.dma_start(picks[:], offs2)
-        gain_t = sb.tile([P, PACK], F32, name="gain_t")
-        nc.gpsimd.dma_start(gain_t[:], gain.rearrange("(p t) o -> p (t o)", t=PACK))
+        wor_raw = load_halves(wor, "wor_raw")
         rs_t = sb.tile([P, PACK], F32, name="rs_t")
-        nc.gpsimd.dma_start(rs_t[:], rs.rearrange("(p t) o -> p (t o)", t=PACK))
-        pb_row = sb.tile([P, M], F32, name="pb_row")
-        nc.sync.dma_start(pb_row[:], pb[0].partition_broadcast(P))
-        wor_rows = wor.rearrange("(p j) c -> p j c", j=PACK)
-        wor_raw = []
-        for h in range(2):
-            part = sb.tile([P, PACK, F // 2], F32, name="wor_raw%d" % h)
-            nc.sync.dma_start(part[:], wor_rows[:, :, h * (F // 2) : (h + 1) * (F // 2)])
-            wor_raw.append(part)
+        nc.sync.dma_start(rs_t[:], rs.rearrange("(p t) o -> p (t o)", t=PACK))
         res_t = sb.tile([P, PACK, M], F32, name="res_t")
         nc.sync.dma_start(res_t[:], res.rearrange("(p t) m -> p t m", t=PACK))
 
@@ -67,32 +73,37 @@ def tile_attend_chpickscaled_pl_kernel(tc, tab_words, tab_scales, w1, gain, pb, 
         nc.scalar.activation(warm2[:], warm[:], ACT.Abs_reciprocal_sqrt)
 
 
+        ident = sb.tile([P, P], F32, name="ident")
+        make_identity(nc, ident[:])
+        pb_ps = bank(7, M)
+        nc.tensor.transpose(pb_ps[:], pb_col[:].to_broadcast([P, P]), ident[:])
+        pb_row = sb.tile([P, M], F32, name="pb_row")
+
         g_s = sb.tile([P, J], U8, name="g_s", align_bytes=64)
         nc.vector.tensor_copy(g_s[:], tab_s[:].indirect(slots[:]))
+        g_w = sb.tile([P, J], U32, name="g_w", align_bytes=64)
+        nc.vector.tensor_copy(g_w[:], tab_w[:].bitcast(U32).indirect(slots[:]))
 
         w1_b = sb.tile([P, PACK, P, PACK], BF16, name="w1_b", align_bytes=64)
-        src = w1_raw[:].rearrange("p j (m t) -> p m j t", t=PACK)
-        dst = w1_b[:].rearrange("p t m j -> p m j t")
-        nc.vector.tensor_copy(dst[:, :W1_VECTOR_COLS], src[:, :W1_VECTOR_COLS])
-        nc.scalar.copy(dst[:, W1_VECTOR_COLS:], src[:, W1_VECTOR_COLS:])
+        for h in range(2):
+            src = w1_raw[h][:].rearrange("p j (m t) -> p m j t", t=PACK)
+            dst = w1_b[:].rearrange("p t m j -> p m j t")[:, h * P // 2 : (h + 1) * P // 2]
+            nc.vector.tensor_copy(dst[:, :W1_VECTOR_COLS], src[:, :W1_VECTOR_COLS])
+            nc.scalar.copy(dst[:, W1_VECTOR_COLS:], src[:, W1_VECTOR_COLS:])
+        nc.scalar.copy(pb_row[:], pb_ps[:])
         w1_c = sb.tile([P, R], U32, name="w1_c", align_bytes=64)
         w1_s = sb.tile([P, R], U8, name="w1_s", align_bytes=64)
-        nc.vector.quantize_mx(w1_c[:].bitcast(FP8X4), w1_s[:], w1_b[:].rearrange("p t m j -> p (t m j)"))
-
-        g_w = []
-        for h in range(2):
-            part = sb.tile([P, HALF], U32, name="g_w%d" % h, align_bytes=64)
-            nc.vector.tensor_copy(part[:], tab_w[:].bitcast(U32).indirect(slots[:, h * HALF // 16 : (h + 1) * HALF // 16]))
-            g_w.append(part)
-
         h1 = [sb.tile([P, J], F32, name="h1_%d" % t) for t in range(PACK)]
-        order = [(0, 0), (1, 0), (0, 1), (1, 1), (2, 0), (2, 1), (3, 0), (3, 1)]
-        for t, h in order:
-            acc = bank(2 * t + h, HALF)
-            nc.tensor.matmul_mx(
-                acc[:], lhsT=w1_c[:, t * P : (t + 1) * P].bitcast(FP8X4), lhsT_scale=w1_s[:, t * P : (t + 1) * P],
-                rhs=g_w[h][:].bitcast(FP8X4), rhs_scale=g_s[:, h * HALF : (h + 1) * HALF], start=True, stop=True)
-            nc.scalar.activation(h1[t][:, h * HALF : (h + 1) * HALF], acc[:], ACT.Copy, scale=gain_t[:, t : t + 1])
+        for t in range(PACK):
+            cols = slice(t * P, (t + 1) * P)
+            nc.vector.quantize_mx(w1_c[:, cols].bitcast(FP8X4), w1_s[:, cols], w1_b[:, t].rearrange("p m j -> p (m j)"))
+            for h in range(2):
+                js = slice(h * HALF, (h + 1) * HALF)
+                acc = bank(2 * t + h, HALF)
+                nc.tensor.matmul_mx(
+                    acc[:], lhsT=w1_c[:, cols].bitcast(FP8X4), lhsT_scale=w1_s[:, cols],
+                    rhs=g_w[:, js].bitcast(FP8X4), rhs_scale=g_s[:, js], start=True, stop=True)
+                nc.scalar.activation(h1[t][:, js], acc[:], ACT.Copy, scale=gain_t[:, t : t + 1])
 
         wor_b = sb.tile([P, PACK, P, PACK], BF16, name="wor_b", align_bytes=64)
         wdst = wor_b[:].rearrange("p t m j -> p m j t")
@@ -101,20 +112,19 @@ def tile_attend_chpickscaled_pl_kernel(tc, tab_words, tab_scales, w1, gain, pb, 
         s = sb.tile([P, PACK, M], F32, name="s")
         sq_head = sb.tile([P, PACK - 1, M], F32, name="sq_head")
         sq_last = wor_b[:].rearrange("p t m j -> p t (m j)")[:, 0:1, 2 * M :].bitcast(F32)
-        ssum = sb.tile([P, G, PACK], F32, name="ssum")
+        ssum = sb.tile([P, PACK, G], F32, name="ssum")
         for t in range(PACK):
             nc.vector.tensor_tensor(s[:, t, :], h1[t][:].indirect(picks[:]), pb_row[:], ALU.add)
         for ts, sq in ((slice(0, PACK - 1), sq_head[:]), (slice(PACK - 1, PACK), sq_last)):
             nc.scalar.activation(sq, s[:, ts, :], ACT.Square)
-            nc.vector.tensor_reduce(ssum[:].rearrange("p g t -> p t g")[:, ts], sq.rearrange("p t (g i) -> p t g i", i=GROUP), AX.X, ALU.add)
-        rinv = sb.tile([P, G, PACK], F32, name="rinv")
+            nc.vector.tensor_reduce(ssum[:, ts], sq.rearrange("p t (g i) -> p t g i", i=GROUP), AX.X, ALU.add)
+        rinv = sb.tile([P, PACK, G], F32, name="rinv")
         nc.scalar.activation(rinv[:], ssum[:], ACT.Abs_reciprocal_sqrt, bias=0.1, scale=1.0 / GROUP)
-
-        z = sb.tile([P, M, PACK], F32, name="z")
+        z = sb.tile([P, PACK, M], F32, name="z")
         nc.vector.tensor_tensor(
-            z[:].rearrange("p (g i) t -> p g i t", i=GROUP),
-            s[:].rearrange("p t (g i) -> p g i t", i=GROUP),
-            rinv[:].unsqueeze(2).to_broadcast([P, G, GROUP, PACK]), ALU.mult)
+            z[:].rearrange("p t (g i) -> p (t g) i", i=GROUP),
+            s[:].rearrange("p t (g i) -> p (t g) i", i=GROUP),
+            rinv[:].rearrange("p t g -> p (t g)").unsqueeze(2).to_broadcast([P, PACK * G, GROUP]), ALU.mult)
 
         nc.vector.tensor_copy(wdst[:, P // 2 :], wor_raw[1][:].rearrange("p j (m t) -> p m j t", t=PACK))
         wor_c = sb.tile([P, F], U32, name="wor_c", align_bytes=64)
@@ -126,7 +136,8 @@ def tile_attend_chpickscaled_pl_kernel(tc, tab_words, tab_scales, w1, gain, pb, 
         fo_b = sb.tile([P, M, PACK], BF16, name="fo_b", align_bytes=64)
         for h in range(2):
             ms = slice(h * M // 2, (h + 1) * M // 2)
-            nc.scalar.activation(u[:, ms, :], z[:, ms, :], ACT.Silu)
+            nc.scalar.activation(
+                u[:, ms, :].rearrange("p (c i) t -> p c t i", i=4), z[:, :, ms].rearrange("p t (c i) -> p c t i", i=4), ACT.Silu)
             nc.vector.tensor_tensor(fo_b[:, ms, :], u[:, ms, :], rs_t[:].unsqueeze(1).to_broadcast([P, M // 2, PACK]), ALU.mult)
         fo_c = sb.tile([P, M], U32, name="fo_c", align_bytes=64)
         fo_s = sb.tile([P, M], U8, name="fo_s", align_bytes=64)

@@ -21,7 +21,6 @@ P = 128
 PACK = 4
 HALF = J // 2
 GROUP = M // G
-W1_VECTOR_COLS = 40
 
 
 def tile_attend_chpickscaled_pl_kernel(tc, tab_words, tab_scales, w1, gain, pb, rs, wor, res, offs, offs2, out_0, out_1, out_2):
@@ -33,13 +32,13 @@ def tile_attend_chpickscaled_pl_kernel(tc, tab_words, tab_scales, w1, gain, pb, 
         def bank(b, cols):
             return ps.tile([P, cols], F32, name="bank%d" % b, tag="bank%d" % b)
 
+        tab_w = sb.tile([P, T], I32, name="tab_w", align_bytes=64)
+        words_hbm = tab_words[0].rearrange("p n t -> p (n t)").bitcast(I32)
+        nc.sync.dma_start(tab_w[:, : T // 2], words_hbm[:, : T // 2])
         slots = sb.tile([P, J // 16], U16, name="slots")
         nc.sync.dma_start(slots[:], offs)
         tab_s = sb.tile([P, T], U8, name="tab_s", align_bytes=64)
         nc.vector.memset(tab_s[:].bitcast(I32), 0)
-        tab_w = sb.tile([P, T], I32, name="tab_w", align_bytes=64)
-        words_hbm = tab_words[0].rearrange("p n t -> p (n t)").bitcast(I32)
-        nc.sync.dma_start(tab_w[:, : T // 2], words_hbm[:, : T // 2])
         for q in range(4):
             nc.sync.dma_start(tab_s[32 * q : 32 * q + 4, :].bitcast(I32), tab_scales[0, 4 * q : 4 * q + 4, :].bitcast(I32))
         nc.sync.dma_start(tab_w[:, T // 2 :], words_hbm[:, T // 2 :])
@@ -88,8 +87,8 @@ def tile_attend_chpickscaled_pl_kernel(tc, tab_words, tab_scales, w1, gain, pb, 
         for h in range(2):
             src = w1_raw[h][:].rearrange("p j (m t) -> p m j t", t=PACK)
             dst = w1_b[:].rearrange("p t m j -> p m j t")[:, h * P // 2 : (h + 1) * P // 2]
-            nc.vector.tensor_copy(dst[:, :W1_VECTOR_COLS], src[:, :W1_VECTOR_COLS])
-            nc.scalar.copy(dst[:, W1_VECTOR_COLS:], src[:, W1_VECTOR_COLS:])
+            nc.vector.tensor_copy(dst[:, :, :, :2], src[:, :, :, :2])
+            nc.scalar.copy(dst[:, :, :, 2:], src[:, :, :, 2:])
         nc.scalar.copy(pb_row[:], pb_ps[:])
         w1_c = sb.tile([P, R], U32, name="w1_c", align_bytes=64)
         w1_s = sb.tile([P, R], U8, name="w1_s", align_bytes=64)
@@ -110,14 +109,17 @@ def tile_attend_chpickscaled_pl_kernel(tc, tab_words, tab_scales, w1, gain, pb, 
         nc.vector.tensor_copy(wdst[:, : P // 2], wor_raw[0][:].rearrange("p j (m t) -> p m j t", t=PACK))
 
         s = sb.tile([P, PACK, M], F32, name="s")
-        sq_head = sb.tile([P, PACK - 1, M], F32, name="sq_head")
-        sq_last = wor_b[:].rearrange("p t m j -> p t (m j)")[:, 0:1, 2 * M :].bitcast(F32)
+        sq = sb.tile([P, PACK - 1, M], F32, name="sq")
+        sq_last = wor_b[:].rearrange("p t m j -> p (t m j)")[:, 2 * M : 4 * M].bitcast(F32)
         ssum = sb.tile([P, PACK, G], F32, name="ssum")
         for t in range(PACK):
             nc.vector.tensor_tensor(s[:, t, :], h1[t][:].indirect(picks[:]), pb_row[:], ALU.add)
-        for ts, sq in ((slice(0, PACK - 1), sq_head[:]), (slice(PACK - 1, PACK), sq_last)):
-            nc.scalar.activation(sq, s[:, ts, :], ACT.Square)
-            nc.vector.tensor_reduce(ssum[:, ts], sq.rearrange("p t (g i) -> p t g i", i=GROUP), AX.X, ALU.add)
+        nc.scalar.activation(sq[:, :2], s[:, :2], ACT.Square)
+        nc.scalar.activation(sq[:, 2], s[:, 2], ACT.Square)
+        nc.vector.tensor_reduce(ssum[:, :2], sq[:, :2].rearrange("p t (g i) -> p t g i", i=GROUP), AX.X, ALU.add)
+        nc.vector.tensor_tensor(sq_last, s[:, 3], s[:, 3], ALU.mult)
+        nc.vector.tensor_reduce(ssum[:, 2], sq[:, 2].rearrange("p (g i) -> p g i", i=GROUP), AX.X, ALU.add)
+        nc.vector.tensor_reduce(ssum[:, 3], sq_last.rearrange("p (g i) -> p g i", i=GROUP), AX.X, ALU.add)
         rinv = sb.tile([P, PACK, G], F32, name="rinv")
         nc.scalar.activation(rinv[:], ssum[:], ACT.Abs_reciprocal_sqrt, bias=0.1, scale=1.0 / GROUP)
         z = sb.tile([P, PACK, M], F32, name="z")
@@ -134,11 +136,10 @@ def tile_attend_chpickscaled_pl_kernel(tc, tab_words, tab_scales, w1, gain, pb, 
 
         u = sb.tile([P, M, PACK], F32, name="u")
         fo_b = sb.tile([P, M, PACK], BF16, name="fo_b", align_bytes=64)
-        for h in range(2):
-            ms = slice(h * M // 2, (h + 1) * M // 2)
+        for ms in (slice(0, 48), slice(48, 96), slice(96, M)):
             nc.scalar.activation(
                 u[:, ms, :].rearrange("p (c i) t -> p c t i", i=4), z[:, :, ms].rearrange("p t (c i) -> p c t i", i=4), ACT.Silu)
-            nc.vector.tensor_tensor(fo_b[:, ms, :], u[:, ms, :], rs_t[:].unsqueeze(1).to_broadcast([P, M // 2, PACK]), ALU.mult)
+            nc.vector.tensor_tensor(fo_b[:, ms, :], u[:, ms, :], rs_t[:].unsqueeze(1).to_broadcast([P, ms.stop - ms.start, PACK]), ALU.mult)
         fo_c = sb.tile([P, M], U32, name="fo_c", align_bytes=64)
         fo_s = sb.tile([P, M], U8, name="fo_s", align_bytes=64)
         nc.vector.quantize_mx(fo_c[:].bitcast(FP8X4), fo_s[:], fo_b[:].rearrange("p m t -> p (m t)"))
@@ -150,11 +151,13 @@ def tile_attend_chpickscaled_pl_kernel(tc, tab_words, tab_scales, w1, gain, pb, 
                 acc[:], lhsT=wor_c[:, t * P : (t + 1) * P].bitcast(FP8X4), lhsT_scale=wor_s[:, t * P : (t + 1) * P],
                 rhs=fo_c[:].bitcast(FP8X4), rhs_scale=fo_s[:], start=True, stop=True)
             nc.vector.tensor_tensor(y[:, t, :], acc[:], res_t[:, t, :], ALU.add)
-        nc.scalar.dma_start(out_0.rearrange("(p t) m -> p t m", t=PACK), y[:])
+        nc.sync.dma_start(out_0.rearrange("(p t) m -> p t m", t=PACK), y[:])
 
         y_b = sb.tile([P, M, PACK], BF16, name="y_b", align_bytes=64)
-        nc.vector.tensor_copy(
-            y_b[:].rearrange("p (c i) t -> p c t i", i=4), y[:].rearrange("p t (c i) -> p c t i", i=4))
+        y_dst = y_b[:].rearrange("p (c i) t -> p c t i", i=4)
+        y_src = y[:].rearrange("p t (c i) -> p c t i", i=4)
+        nc.vector.tensor_copy(y_dst[:, :20], y_src[:, :20])
+        nc.scalar.copy(y_dst[:, 20:], y_src[:, 20:])
         y_c = sb.tile([P, M], U32, name="y_c", align_bytes=64)
         y_s = sb.tile([P, M], U8, name="y_s", align_bytes=64)
         nc.vector.quantize_mx(y_c[:].bitcast(FP8X4), y_s[:], y_b[:].rearrange("p m t -> p (m t)"))

@@ -43,33 +43,30 @@ def tile_attend_chpickscaled_pl_kernel(tc, tab_words, tab_scales, w1, gain, pb, 
             nc.sync.dma_start(tab_s[32 * q : 32 * q + 4, :].bitcast(I32), tab_scales[0, 4 * q : 4 * q + 4, :].bitcast(I32))
         nc.sync.dma_start(tab_w[:, T // 2 :], words_hbm[:, T // 2 :])
 
-        def load_halves(w, name):
-            rows = w.rearrange("(p j) c -> p j c", j=PACK)
-            halves = []
-            for h in range(2):
-                part = sb.tile([P, PACK, R // 2], F32, name="%s%d" % (name, h))
-                nc.sync.dma_start(part[:], rows[:, :, h * (R // 2) : (h + 1) * (R // 2)])
-                halves.append(part)
-            return halves
+        def load_half(w, h, name):
+            part = sb.tile([P, PACK, R // 2], F32, name="%s%d" % (name, h))
+            nc.sync.dma_start(part[:], w.rearrange("(p j) c -> p j c", j=PACK)[:, :, h * (R // 2) : (h + 1) * (R // 2)])
+            return part
 
-        w1_raw = load_halves(w1, "w1_raw")
+        w1_raw = [load_half(w1, h, "w1_raw") for h in range(2)]
         pb_col = sb.tile([P, 1], F32, name="pb_col")
         with nc.allow_non_contiguous_dma(reason="one value a partition"):
             nc.sync.dma_start(pb_col[:], pb.rearrange("o m -> m o"))
+        wor_raw = [load_half(wor, 0, "wor_raw")]
         gain_t = sb.tile([P, PACK], F32, name="gain_t")
         nc.sync.dma_start(gain_t[:], gain.rearrange("(p t) o -> p (t o)", t=PACK))
         picks = sb.tile([P, M // 16], U16, name="picks")
         nc.sync.dma_start(picks[:], offs2)
-        wor_raw = load_halves(wor, "wor_raw")
+        wor_raw.append(load_half(wor, 1, "wor_raw"))
         rs_t = sb.tile([P, PACK], F32, name="rs_t")
         nc.sync.dma_start(rs_t[:], rs.rearrange("(p t) o -> p (t o)", t=PACK))
         res_t = sb.tile([P, PACK, M], F32, name="res_t")
         nc.sync.dma_start(res_t[:], res.rearrange("(p t) m -> p t m", t=PACK))
 
-        warm = sb.tile([P, 1], F32, name="warm")
-        nc.vector.memset(warm[:], 1.0)
-        warm2 = sb.tile([P, 1], F32, name="warm2")
-        nc.scalar.activation(warm2[:], warm[:], ACT.Abs_reciprocal_sqrt)
+        hundred = sb.tile([P, 1], F32, name="hundred")
+        nc.vector.memset(hundred[:], 100.0)
+        eps = sb.tile([P, 1], F32, name="eps")
+        nc.scalar.activation(eps[:], hundred[:], ACT.Abs_reciprocal_sqrt)
 
 
         ident = sb.tile([P, P], F32, name="ident")
@@ -105,8 +102,8 @@ def tile_attend_chpickscaled_pl_kernel(tc, tab_words, tab_scales, w1, gain, pb, 
                 nc.scalar.activation(h1[t][:, js], acc[:], ACT.Copy, scale=gain_t[:, t : t + 1])
 
         wor_b = sb.tile([P, PACK, P, PACK], BF16, name="wor_b", align_bytes=64)
-        wdst = wor_b[:].rearrange("p t m j -> p m j t")
-        nc.vector.tensor_copy(wdst[:, : P // 2], wor_raw[0][:].rearrange("p j (m t) -> p m j t", t=PACK))
+        wdst = wor_b[:].rearrange("p (a b) m j -> p a m j b", b=2)
+        nc.vector.tensor_copy(wdst[:, :, : P // 2], wor_raw[0][:].rearrange("p j (m a b) -> p a m j b", a=2, b=2))
 
         s = sb.tile([P, PACK, M], F32, name="s")
         sq = sb.tile([P, PACK - 1, M], F32, name="sq")
@@ -121,14 +118,14 @@ def tile_attend_chpickscaled_pl_kernel(tc, tab_words, tab_scales, w1, gain, pb, 
         nc.vector.tensor_reduce(ssum[:, 2], sq[:, 2].rearrange("p (g i) -> p g i", i=GROUP), AX.X, ALU.add)
         nc.vector.tensor_reduce(ssum[:, 3], sq_last.rearrange("p (g i) -> p g i", i=GROUP), AX.X, ALU.add)
         rinv = sb.tile([P, PACK, G], F32, name="rinv")
-        nc.scalar.activation(rinv[:], ssum[:], ACT.Abs_reciprocal_sqrt, bias=0.1, scale=1.0 / GROUP)
+        nc.scalar.activation(rinv[:], ssum[:], ACT.Abs_reciprocal_sqrt, bias=eps[:], scale=1.0 / GROUP)
         z = sb.tile([P, PACK, M], F32, name="z")
         nc.vector.tensor_tensor(
             z[:].rearrange("p t (g i) -> p (t g) i", i=GROUP),
             s[:].rearrange("p t (g i) -> p (t g) i", i=GROUP),
             rinv[:].rearrange("p t g -> p (t g)").unsqueeze(2).to_broadcast([P, PACK * G, GROUP]), ALU.mult)
 
-        nc.vector.tensor_copy(wdst[:, P // 2 :], wor_raw[1][:].rearrange("p j (m t) -> p m j t", t=PACK))
+        nc.vector.tensor_copy(wdst[:, :, P // 2 :], wor_raw[1][:].rearrange("p j (m a b) -> p a m j b", a=2, b=2))
         wor_c = sb.tile([P, F], U32, name="wor_c", align_bytes=64)
         wor_s = sb.tile([P, F], U8, name="wor_s", align_bytes=64)
         nc.vector.quantize_mx(wor_c[:].bitcast(FP8X4), wor_s[:], wor_b[:].rearrange("p t m j -> p (t m j)"))
@@ -138,7 +135,7 @@ def tile_attend_chpickscaled_pl_kernel(tc, tab_words, tab_scales, w1, gain, pb, 
         fo_b = sb.tile([P, M, PACK], BF16, name="fo_b", align_bytes=64)
         for ms in (slice(0, 48), slice(48, 96), slice(96, M)):
             nc.scalar.activation(
-                u[:, ms, :].rearrange("p (c i) t -> p c t i", i=4), z[:, :, ms].rearrange("p t (c i) -> p c t i", i=4), ACT.Silu)
+                u[:, ms, :].rearrange("p (c i) t -> p c t i", i=2), z[:, :, ms].rearrange("p t (c i) -> p c t i", i=2), ACT.Silu)
             nc.vector.tensor_tensor(fo_b[:, ms, :], u[:, ms, :], rs_t[:].unsqueeze(1).to_broadcast([P, ms.stop - ms.start, PACK]), ALU.mult)
         fo_c = sb.tile([P, M], U32, name="fo_c", align_bytes=64)
         fo_s = sb.tile([P, M], U8, name="fo_s", align_bytes=64)

@@ -32,36 +32,27 @@ def tile_attend_chpickscaled_pl_kernel(tc, tab_words, tab_scales, w1, gain, pb, 
         def bank(b, cols):
             return ps.tile([P, cols], F32, name="bank%d" % b, tag="bank%d" % b)
 
-        tab_w = sb.tile([P, T], I32, name="tab_w", align_bytes=64)
+        tab_w = sb.tile([P, T], I32, name="tab_w", tag="tab_w", align_bytes=64)
         words_hbm = tab_words[0].rearrange("p n t -> p (n t)").bitcast(I32)
-        nc.sync.dma_start(tab_w[:, : T // 2], words_hbm[:, : T // 2])
+        nc.sync.dma_start(tab_w[:, : 3 * T // 8], words_hbm[:, : 3 * T // 8])
         slots = sb.tile([P, J // 16], U16, name="slots")
         nc.sync.dma_start(slots[:], offs)
-        tab_s = sb.tile([P, T], U8, name="tab_s", align_bytes=64)
+        tab_s = sb.tile([P, T], U8, name="tab_s", tag="tab_s", align_bytes=64)
         nc.vector.memset(tab_s[:].bitcast(I32), 0)
-        for q in range(4):
-            nc.sync.dma_start(tab_s[32 * q : 32 * q + 4, :].bitcast(I32), tab_scales[0, 4 * q : 4 * q + 4, :].bitcast(I32))
-        nc.sync.dma_start(tab_w[:, T // 2 :], words_hbm[:, T // 2 :])
+        nc.sync.dma_start(tab_s[0:P:8, :].bitcast(I32), tab_scales[0].bitcast(I32))
+        nc.sync.dma_start(tab_w[:, 3 * T // 8 :], words_hbm[:, 3 * T // 8 :])
 
-        def load_half(w, h, name):
-            part = sb.tile([P, PACK, R // 2], F32, name="%s%d" % (name, h))
+        def load_half(w, h, name, tag):
+            part = sb.tile([P, PACK, R // 2], F32, name=name, tag=tag, align_bytes=64)
             nc.sync.dma_start(part[:], w.rearrange("(p j) c -> p j c", j=PACK)[:, :, h * (R // 2) : (h + 1) * (R // 2)])
             return part
 
-        w1_raw = [load_half(w1, h, "w1_raw") for h in range(2)]
-        pb_col = sb.tile([P, 1], F32, name="pb_col")
+        w1_raw = [load_half(w1, h, "w1_raw%d" % h, "w1_raw%d" % h) for h in range(2)]
+        pb_col = sb.tile([P, 1], F32, name="pb_col", tag="pb_col")
         with nc.allow_non_contiguous_dma(reason="one value a partition"):
             nc.sync.dma_start(pb_col[:], pb.rearrange("o m -> m o"))
-        wor_raw = [load_half(wor, 0, "wor_raw")]
-        gain_t = sb.tile([P, PACK], F32, name="gain_t")
-        nc.sync.dma_start(gain_t[:], gain.rearrange("(p t) o -> p (t o)", t=PACK))
         picks = sb.tile([P, M // 16], U16, name="picks")
         nc.sync.dma_start(picks[:], offs2)
-        wor_raw.append(load_half(wor, 1, "wor_raw"))
-        rs_t = sb.tile([P, PACK], F32, name="rs_t")
-        nc.sync.dma_start(rs_t[:], rs.rearrange("(p t) o -> p (t o)", t=PACK))
-        res_t = sb.tile([P, PACK, M], F32, name="res_t")
-        nc.sync.dma_start(res_t[:], res.rearrange("(p t) m -> p t m", t=PACK))
 
         hundred = sb.tile([P, 1], F32, name="hundred")
         nc.vector.memset(hundred[:], 100.0)
@@ -75,10 +66,18 @@ def tile_attend_chpickscaled_pl_kernel(tc, tab_words, tab_scales, w1, gain, pb, 
         nc.tensor.transpose(pb_ps[:], pb_col[:].to_broadcast([P, P]), ident[:])
         pb_row = sb.tile([P, M], F32, name="pb_row")
 
+        g_rows = sb.tile([P, J], U8, name="g_rows", align_bytes=64)
+        nc.vector.tensor_copy(g_rows[:], tab_s[:].indirect(slots[:]))
+        gain_t = sb.tile([P, PACK], F32, name="gain_t", tag="tab_s", align_bytes=64)
+        nc.sync.dma_start(gain_t[:], gain.rearrange("(p t) o -> p (t o)", t=PACK))
         g_s = sb.tile([P, J], U8, name="g_s", align_bytes=64)
-        nc.vector.tensor_copy(g_s[:], tab_s[:].indirect(slots[:]))
+        nc.vector.tensor_copy(g_s[:].bitcast(I32), g_rows[:].bitcast(I32))
+        for i in range(1, 4):
+            nc.scalar.dma_start(g_s[i:P:32, :].bitcast(I32), g_rows[8 * i : P : 32, :].bitcast(I32))
         g_w = sb.tile([P, J], U32, name="g_w", align_bytes=64)
         nc.vector.tensor_copy(g_w[:], tab_w[:].bitcast(U32).indirect(slots[:]))
+
+        wor_raw = [load_half(wor, 0, "wor_raw0", "tab_w")]
 
         w1_b = sb.tile([P, PACK, P, PACK], BF16, name="w1_b", align_bytes=64)
         for h in range(2):
@@ -87,6 +86,11 @@ def tile_attend_chpickscaled_pl_kernel(tc, tab_words, tab_scales, w1, gain, pb, 
             nc.vector.tensor_copy(dst[:, :, :, :2], src[:, :, :, :2])
             nc.scalar.copy(dst[:, :, :, 2:], src[:, :, :, 2:])
         nc.scalar.copy(pb_row[:], pb_ps[:])
+        wor_raw.append(load_half(wor, 1, "wor_raw1", "w1_raw0"))
+        rs_t = sb.tile([P, PACK], F32, name="rs_t", tag="pb_col")
+        nc.sync.dma_start(rs_t[:], rs.rearrange("(p t) o -> p (t o)", t=PACK))
+        res_t = sb.tile([P, PACK, M], F32, name="res_t", tag="w1_raw1", align_bytes=64)
+        nc.sync.dma_start(res_t[:], res.rearrange("(p t) m -> p t m", t=PACK))
         w1_c = sb.tile([P, R], U32, name="w1_c", align_bytes=64)
         w1_s = sb.tile([P, R], U8, name="w1_s", align_bytes=64)
         h1 = [sb.tile([P, J], F32, name="h1_%d" % t) for t in range(PACK)]

from contextlib import ExitStack

import concourse.mybir as mybir
from concourse.masks import make_identity

K, R, F, T, J, M, G = 512, 512, 512, 2048, 512, 128, 16
FLOPS = 2 * K * R * J + 2 * R * F * M

F32 = mybir.dt.float32
BF16 = mybir.dt.bfloat16
I32 = mybir.dt.int32
U32 = mybir.dt.uint32
U16 = mybir.dt.uint16
U8 = mybir.dt.uint8
FP8X4 = mybir.dt.float8_e4m3fn_x4
ACT = mybir.ActivationFunctionType
ALU = mybir.AluOpType
AX = mybir.AxisListType

P = 128
PACK = 4
HALF = J // 2
GROUP = M // G


def tile_attend_chpickscaled_pl_kernel(tc, tab_words, tab_scales, w1, gain, pb, rs, wor, res, offs, offs2, out_0, out_1, out_2):
    nc = tc.nc
    with ExitStack() as ctx:
        sb = ctx.enter_context(tc.tile_pool(name="sb", bufs=1))
        ps = ctx.enter_context(tc.psum_pool(name="ps", bufs=1))

        def bank(b, cols):
            return ps.tile([P, cols], F32, name="bank%d" % b, tag="bank%d" % b)

        tab_w = sb.tile([P, T], I32, name="tab_w", tag="tab_w", align_bytes=64)
        words_hbm = tab_words[0].rearrange("p n t -> p (n t)").bitcast(I32)
        nc.sync.dma_start(tab_w[:, : 3 * T // 8], words_hbm[:, : 3 * T // 8])
        slots = sb.tile([P, J // 16], U16, name="slots")
        nc.sync.dma_start(slots[:], offs)
        tab_s = sb.tile([P, T], U8, name="tab_s", tag="tab_s", align_bytes=64)
        nc.vector.memset(tab_s[:].bitcast(I32), 0)
        nc.sync.dma_start(tab_s[0:P:8, :].bitcast(I32), tab_scales[0].bitcast(I32))
        nc.sync.dma_start(tab_w[:, 3 * T // 8 :], words_hbm[:, 3 * T // 8 :])

        def load_half(w, h, name, tag):
            part = sb.tile([P, PACK, R // 2], F32, name=name, tag=tag, align_bytes=64)
            nc.sync.dma_start(part[:], w.rearrange("(p j) c -> p j c", j=PACK)[:, :, h * (R // 2) : (h + 1) * (R // 2)])
            return part

        w1_raw = [load_half(w1, h, "w1_raw%d" % h, "w1_raw%d" % h) for h in range(2)]
        pb_col = sb.tile([P, 1], F32, name="pb_col", tag="pb_col")
        with nc.allow_non_contiguous_dma(reason="one value a partition"):
            nc.sync.dma_start(pb_col[:], pb.rearrange("o m -> m o"))
        picks = sb.tile([P, M // 16], U16, name="picks")
        nc.sync.dma_start(picks[:], offs2)

        hundred = sb.tile([P, 1], F32, name="hundred")
        nc.vector.memset(hundred[:], 100.0)
        eps = sb.tile([P, 1], F32, name="eps")
        nc.scalar.activation(eps[:], hundred[:], ACT.Abs_reciprocal_sqrt)


        ident = sb.tile([P, P], F32, name="ident")
        make_identity(nc, ident[:])
        pb_ps = bank(7, M)
        nc.tensor.transpose(pb_ps[:], pb_col[:].to_broadcast([P, P]), ident[:])
        pb_row = sb.tile([P, M], F32, name="pb_row")

        g_rows = sb.tile([P, J], U8, name="g_rows", align_bytes=64)
        nc.vector.tensor_copy(g_rows[:], tab_s[:].indirect(slots[:]))
        gain_t = sb.tile([P, PACK], F32, name="gain_t", tag="tab_s", align_bytes=64)
        nc.sync.dma_start(gain_t[:], gain.rearrange("(p t) o -> p (t o)", t=PACK))
        g_s = sb.tile([P, J], U8, name="g_s", align_bytes=64)
        nc.vector.tensor_copy(g_s[:].bitcast(I32), g_rows[:].bitcast(I32))
        for i in range(1, 4):
            nc.scalar.dma_start(g_s[i:P:32, :].bitcast(I32), g_rows[8 * i : P : 32, :].bitcast(I32))
        g_w = sb.tile([P, J], U32, name="g_w", align_bytes=64)
        nc.vector.tensor_copy(g_w[:], tab_w[:].bitcast(U32).indirect(slots[:]))

        wor_raw = [load_half(wor, 0, "wor_raw0", "tab_w")]

        w1_b = sb.tile([P, PACK, P, PACK], BF16, name="w1_b", align_bytes=64)
        for h in range(2):
            src = w1_raw[h][:].rearrange("p j (m t) -> p m j t", t=PACK)
            dst = w1_b[:].rearrange("p t m j -> p m j t")[:, h * P // 2 : (h + 1) * P // 2]
            nc.vector.tensor_copy(dst[:, :, :, :2], src[:, :, :, :2])
            nc.scalar.copy(dst[:, :, :, 2:], src[:, :, :, 2:])
        nc.scalar.copy(pb_row[:], pb_ps[:])
        wor_raw.append(load_half(wor, 1, "wor_raw1", "w1_raw0"))
        rs_t = sb.tile([P, PACK], F32, name="rs_t", tag="pb_col")
        nc.sync.dma_start(rs_t[:], rs.rearrange("(p t) o -> p (t o)", t=PACK))
        res_t = sb.tile([P, PACK, M], F32, name="res_t", tag="w1_raw1", align_bytes=64)
        nc.sync.dma_start(res_t[:], res.rearrange("(p t) m -> p t m", t=PACK))
        w1_c = sb.tile([P, R], U32, name="w1_c", align_bytes=64)
        w1_s = sb.tile([P, R], U8, name="w1_s", align_bytes=64)
        h1 = [sb.tile([P, J], F32, name="h1_%d" % t) for t in range(PACK)]
        for t in range(PACK):
            cols = slice(t * P, (t + 1) * P)
            nc.vector.quantize_mx(w1_c[:, cols].bitcast(FP8X4), w1_s[:, cols], w1_b[:, t].rearrange("p m j -> p (m j)"))
            for h in range(2):
                js = slice(h * HALF, (h + 1) * HALF)
                acc = bank(2 * t + h, HALF)
                nc.tensor.matmul_mx(
                    acc[:], lhsT=w1_c[:, cols].bitcast(FP8X4), lhsT_scale=w1_s[:, cols],
                    rhs=g_w[:, js].bitcast(FP8X4), rhs_scale=g_s[:, js], start=True, stop=True)
                nc.scalar.activation(h1[t][:, js], acc[:], ACT.Copy, scale=gain_t[:, t : t + 1])

        wor_b = sb.tile([P, PACK, P, PACK], BF16, name="wor_b", align_bytes=64)
        wdst = wor_b[:].rearrange("p (a b) m j -> p a m j b", b=2)
        nc.vector.tensor_copy(wdst[:, :, : P // 2], wor_raw[0][:].rearrange("p j (m a b) -> p a m j b", a=2, b=2))

        s = sb.tile([P, PACK, M], F32, name="s")
        sq = sb.tile([P, PACK - 1, M], F32, name="sq")
        sq_last = wor_b[:].rearrange("p t m j -> p (t m j)")[:, 2 * M : 4 * M].bitcast(F32)
        ssum = sb.tile([P, PACK, G], F32, name="ssum")
        for t in range(PACK):
            nc.vector.tensor_tensor(s[:, t, :], h1[t][:].indirect(picks[:]), pb_row[:], ALU.add)
        nc.scalar.activation(sq[:, :2], s[:, :2], ACT.Square)
        nc.scalar.activation(sq[:, 2], s[:, 2], ACT.Square)
        nc.vector.tensor_reduce(ssum[:, :2], sq[:, :2].rearrange("p t (g i) -> p t g i", i=GROUP), AX.X, ALU.add)
        nc.vector.tensor_tensor(sq_last, s[:, 3], s[:, 3], ALU.mult)
        nc.vector.tensor_reduce(ssum[:, 2], sq[:, 2].rearrange("p (g i) -> p g i", i=GROUP), AX.X, ALU.add)
        nc.vector.tensor_reduce(ssum[:, 3], sq_last.rearrange("p (g i) -> p g i", i=GROUP), AX.X, ALU.add)
        rinv = sb.tile([P, PACK, G], F32, name="rinv")
        nc.scalar.activation(rinv[:], ssum[:], ACT.Abs_reciprocal_sqrt, bias=eps[:], scale=1.0 / GROUP)
        z = sb.tile([P, PACK, M], F32, name="z")
        nc.vector.tensor_tensor(
            z[:].rearrange("p t (g i) -> p (t g) i", i=GROUP),
            s[:].rearrange("p t (g i) -> p (t g) i", i=GROUP),
            rinv[:].rearrange("p t g -> p (t g)").unsqueeze(2).to_broadcast([P, PACK * G, GROUP]), ALU.mult)

        nc.vector.tensor_copy(wdst[:, :, P // 2 :], wor_raw[1][:].rearrange("p j (m a b) -> p a m j b", a=2, b=2))
        wor_c = sb.tile([P, F], U32, name="wor_c", align_bytes=64)
        wor_s = sb.tile([P, F], U8, name="wor_s", align_bytes=64)
        nc.vector.quantize_mx(wor_c[:].bitcast(FP8X4), wor_s[:], wor_b[:].rearrange("p t m j -> p (t m j)"))


        u = sb.tile([P, M, PACK], F32, name="u")
        fo_b = sb.tile([P, M, PACK], BF16, name="fo_b", align_bytes=64)
        for ms in (slice(0, 48), slice(48, 96), slice(96, M)):
            nc.scalar.activation(
                u[:, ms, :].rearrange("p (c i) t -> p c t i", i=2), z[:, :, ms].rearrange("p t (c i) -> p c t i", i=2), ACT.Silu)
            nc.vector.tensor_tensor(fo_b[:, ms, :], u[:, ms, :], rs_t[:].unsqueeze(1).to_broadcast([P, ms.stop - ms.start, PACK]), ALU.mult)
        fo_c = sb.tile([P, M], U32, name="fo_c", align_bytes=64)
        fo_s = sb.tile([P, M], U8, name="fo_s", align_bytes=64)
        nc.vector.quantize_mx(fo_c[:].bitcast(FP8X4), fo_s[:], fo_b[:].rearrange("p m t -> p (m t)"))

        y = sb.tile([P, PACK, M], F32, name="y")
        for t in range(PACK):
            acc = bank(t, M)
            nc.tensor.matmul_mx(
                acc[:], lhsT=wor_c[:, t * P : (t + 1) * P].bitcast(FP8X4), lhsT_scale=wor_s[:, t * P : (t + 1) * P],
                rhs=fo_c[:].bitcast(FP8X4), rhs_scale=fo_s[:], start=True, stop=True)
            nc.vector.tensor_tensor(y[:, t, :], acc[:], res_t[:, t, :], ALU.add)
        nc.sync.dma_start(out_0.rearrange("(p t) m -> p t m", t=PACK), y[:])

        y_b = sb.tile([P, M, PACK], BF16, name="y_b", align_bytes=64)
        y_dst = y_b[:].rearrange("p (c i) t -> p c t i", i=4)
        y_src = y[:].rearrange("p t (c i) -> p c t i", i=4)
        nc.vector.tensor_copy(y_dst[:, :20], y_src[:, :20])
        nc.scalar.copy(y_dst[:, 20:], y_src[:, 20:])
        y_c = sb.tile([P, M], U32, name="y_c", align_bytes=64)
        y_s = sb.tile([P, M], U8, name="y_s", align_bytes=64)
        nc.vector.quantize_mx(y_c[:].bitcast(FP8X4), y_s[:], y_b[:].rearrange("p m t -> p (m t)"))
        nc.sync.dma_start(out_1[0].rearrange("p c r -> p (c r)").bitcast(I32), y_c[:].bitcast(I32))
        for q in range(4):
            eng = nc.sync if q < 2 else nc.scalar
            eng.dma_start(out_2[0, 4 * q : 4 * q + 4, :].bitcast(I32), y_s[32 * q : 32 * q + 4, :].bitcast(I32))
